import numpy as np
import ml_dtypes


def mxq(x, axis, fmt="e4m3"):
    dtype, down = {"e4m3": (ml_dtypes.float8_e4m3fn, 7), "e5m2": (ml_dtypes.float8_e5m2, 14)}[fmt]
    v = np.moveaxis(np.asarray(x, np.float32).astype(ml_dtypes.bfloat16).astype(np.float64), axis, -1)
    blocks = v.reshape(v.shape[:-1] + (-1, 32))
    amax = np.abs(blocks).max(-1, keepdims=True)
    byte = np.maximum(np.where(amax > 0, np.frexp(amax)[1] - 1 + 127, 0) - down, 1)
    scale = np.exp2(byte - 127.0)
    codes = (blocks / scale).astype(np.float32).astype(dtype).astype(np.float64)
    return np.moveaxis((codes * scale).reshape(v.shape), -1, axis)


WIDE = False


def mx_kscale(k):
    if not WIDE:
        return np.ones(k)
    levels = np.array([10, -10, 5, -5, 0])
    if k % 512:
        return np.exp2(np.random.permutation(np.resize(levels, k // 32))).repeat(32)
    a = np.empty((k // 512, 16))
    for p in range(k // 512):
        a[p, :8] = np.random.permutation(np.resize(levels, 8))
        for g in range(8):
            far = levels[np.abs(levels - a[p, g]) >= 10]
            a[p, g + 8] = far[np.random.randint(len(far))]
    return np.exp2(a.ravel()).repeat(32)


def f64(x):
    return np.asarray(x).astype(np.float64)


def striped(idx):
    return np.tile(idx.reshape(-1, 16).T, (8, 1)).astype(np.uint16)


def unstriped(offs):
    return offs[:16].T.reshape(-1).astype(np.int64)


def striped8(idx):
    return np.concatenate([x.reshape(-1, 16).T for x in idx]).astype(np.uint16)


def runs(offs, k):
    lists = np.stack([offs[16 * r : 16 * r + 16].T.reshape(-1) for r in range(8)]).astype(np.int64)
    return lists[np.arange(k) % 512 // 64]


def pack_weight(w):
    k, n = w.shape
    w = f64(np.asarray(w, np.float32).astype(ml_dtypes.bfloat16)).reshape(k // 32, 32, n)
    amax = np.abs(w).max(1)
    byte = np.clip(np.where(amax > 0, np.frexp(amax)[1] - 1 + 127 - 7, 1), 1, 254)
    scaled = (w * np.exp2(127.0 - byte)[:, None, :]).reshape(k, n).astype(np.float32)
    words = np.ascontiguousarray(scaled.reshape(k // 512, 128, 4, n).transpose(0, 1, 3, 2)).astype(ml_dtypes.float8_e4m3fn).view(np.uint8)
    return words, np.ascontiguousarray(byte.astype(np.uint8).reshape(k // 512, 16, n))


def unpack_weight(words, scales):
    g, p, n, _ = words.shape
    vals = np.ascontiguousarray(words).view(ml_dtypes.float8_e4m3fn).astype(np.float64) * np.repeat(np.exp2(scales.astype(np.float64) - 127.0), 8, axis=1)[..., None]
    return vals.transpose(0, 1, 3, 2).reshape(g * 512, n)


def sigmoid(v):
    return 1.0 / (1.0 + np.exp(-np.maximum(v, -700.0)))


K, T, S, N, G, H, W = 512, 2048, 512, 512, 2048, 512, 256


def setup_inputs():
    n = np.random.standard_normal
    s = mx_kscale(K)[:, None]
    u = mx_kscale(S)
    packed_xT = pack_weight(n((K, T)) * s)
    packed_dT = pack_weight(n((K, G)) / s)
    perm = np.stack([np.random.permutation(S) for _ in range(8)])
    return {
        "x_words": packed_xT[0],
        "x_scales": packed_xT[1],
        "d_words": packed_dT[0],
        "d_scales": packed_dT[1],
        "gn": (np.random.uniform(0.5, 1.5, (H, 1)) * u[:, None]).astype(np.float32),
        "w1": (n((H, N)) / np.sqrt(H) / u[:, None]).astype(np.float32),
        "offs": striped(np.random.permutation(T)[:S]),
        "k1": striped8(np.random.randint(0, G, (8, H))),
        "n1": striped8(np.stack([np.random.permutation(S) for _ in range(8)])),
        "n2": striped8(perm[:, :W]),
        "n3": striped8(perm[:, W:]),
    }


def reference(x_words, x_scales, d_words, d_scales, gn, w1, offs, k1, n1, n2, n3):
    d_k1 = unpack_weight(d_words, d_scales)[np.arange(K)[:, None], runs(k1, K)]
    xq = unpack_weight(x_words, x_scales)[:, unstriped(offs)]
    h = 0.0625 * (d_k1.T @ xq)
    z = f64(gn) * (h * (sigmoid(h[np.arange(H)[:, None], runs(n1, H)])))
    h2 = mxq(f64(w1), 0, "e4m3").T @ mxq(z, 0, "e4m3")
    pb = h2[np.arange(N)[:, None], runs(n3, N)]
    pa = h2[np.arange(N)[:, None], runs(n2, N)]
    rb = pb - (0.5 * pa)
    ra = np.sqrt((pa) ** 2 + (pb) ** 2 + 0.25)
    ds = np.zeros((N, S))
    ds[np.arange(N)[:, None], runs(n2, N)] = ra
    out = ds.copy()
    out[np.arange(N)[:, None], runs(n3, N)] = rb
    return out

@@ -1,0 +1,216 @@
+from contextlib import ExitStack
+
+import concourse.mybir as mybir
+
+F32 = mybir.dt.float32
+BF16 = mybir.dt.bfloat16
+I32 = mybir.dt.int32
+U32 = mybir.dt.uint32
+U16 = mybir.dt.uint16
+U8 = mybir.dt.uint8
+FP8X4 = mybir.dt.float8_e4m3fn_x4
+ACT = mybir.ActivationFunctionType
+ALU = mybir.AluOpType
+
+P = 128
+PACK = 4
+TABLE = 2048
+S = 512
+PAIRS = 256
+HALF = 256
+
+FLOPS = 2 * 2 * 512 * 512 * 512
+
+
+def tile_picked_pqlaygatepolar_none_p_kernel(
+    tc, x_words, x_scales, d_words, d_scales, gn, w1, offs, k1, n1, n2, n3, out
+):
+    nc = tc.nc
+    with ExitStack() as ctx:
+        lists = ctx.enter_context(tc.tile_pool(name="lists", bufs=1))
+        keep = ctx.enter_context(tc.tile_pool(name="keep", bufs=1))
+        psum = ctx.enter_context(tc.psum_pool(name="psum", bufs=1))
+
+        k1_t = lists.tile([P, S // 16], U16, name="k1_t")
+        offs_t = lists.tile([P, S // 16], U16, name="offs_t")
+        n1_t = lists.tile([P, S // 16], U16, name="n1_t")
+        n2_t = lists.tile([P, PAIRS // 16], U16, name="n2_t")
+        n3_t = lists.tile([P, PAIRS // 16], U16, name="n3_t")
+
+        d_byte_table = keep.tile([P, TABLE], U8, name="d_byte_table", tag="early2", align_bytes=64)
+        x_byte_table = keep.tile([P, TABLE], U8, name="x_byte_table", align_bytes=64)
+        d_word_table = keep.tile([P, TABLE], U32, name="d_word_table", align_bytes=64)
+        x_word_table = keep.tile([P, TABLE], U32, name="x_word_table", align_bytes=64)
+        planes = keep.tile([P, 2 * S], U8, name="planes", align_bytes=64)
+
+        nc.vector.memset(d_byte_table[:].bitcast(I32), 0)
+        nc.gpsimd.memset(x_byte_table[:, 0 : TABLE // 2].bitcast(I32), 0)
+        nc.vector.memset(x_byte_table[:, TABLE // 2 :].bitcast(I32), 0)
+        nc.gpsimd.memset(planes[:].bitcast(I32), 0)
+
+        nc.sync.dma_start(d_byte_table[0:P:8, :].bitcast(I32), d_scales[0].bitcast(I32))
+        nc.sync.dma_start(x_byte_table[0:P:8, :].bitcast(I32), x_scales[0].bitcast(I32))
+        nc.sync.dma_start(k1_t[:], k1)
+        nc.sync.dma_start(offs_t[:], offs)
+        nc.sync.dma_start(n1_t[:], n1)
+        nc.sync.dma_start(n2_t[:], n2)
+        nc.sync.dma_start(n3_t[:], n3)
+        nc.sync.dma_start(d_word_table[:].bitcast(I32), d_words[0].rearrange("p n t -> p (n t)").bitcast(I32))
+        nc.sync.dma_start(x_word_table[:].bitcast(I32), x_words[0].rearrange("p n t -> p (n t)").bitcast(I32))
+
+        d_bytes = keep.tile([P, S], U8, name="d_bytes", tag="early0", align_bytes=64)
+        x_bytes = keep.tile([P, S], U8, name="x_bytes", tag="early1", align_bytes=64)
+        staged = keep.tile([P, 2 * S], U8, name="staged", align_bytes=64)
+        nc.vector.tensor_copy(d_bytes[:], d_byte_table[:].indirect(k1_t[:]))
+        nc.vector.tensor_copy(x_bytes[:], x_byte_table[:].indirect(offs_t[:]))
+        nc.vector.tensor_copy(
+            staged[:, 0:S].rearrange("p (t m) -> p m t", t=PACK),
+            d_bytes[:].rearrange("p (m t) -> p m t", t=PACK),
+        )
+        nc.vector.tensor_copy(staged[:, S : 2 * S].bitcast(I32), x_bytes[:].bitcast(I32))
+        for q in range(4):
+            (nc.sync if q % 2 == 0 else nc.scalar).dma_start(
+                planes[32 * q : 32 * q + 4, :].bitcast(I32),
+                staged[32 * q : 32 * q + 32 : 8, :].bitcast(I32),
+            )
+
+        w_rows = w1.rearrange("(p j) n -> p j n", j=PACK)
+        w_raw = keep.tile([P, 2, PACK, HALF], F32, name="w_raw", tag="early1", align_bytes=64)
+        for c in range(2):
+            nc.sync.dma_start(w_raw[:, c, :, :], w_rows[:, :, HALF * c : HALF * (c + 1)])
+        gain = keep.tile([P, PACK], F32, name="gain", tag="early2", align_bytes=64)
+        nc.sync.dma_start(gain[:], gn.rearrange("(p t) o -> p (t o)", t=PACK))
+
+        d_picked = keep.tile([P, S], U32, name="d_picked", align_bytes=64)
+        d_dealt = keep.tile([P, S], U32, name="d_dealt", align_bytes=64)
+        nc.vector.tensor_copy(d_picked[:], d_word_table[:].indirect(k1_t[:]))
+        nc.vector.tensor_copy(
+            d_dealt[:].rearrange("p (t m) -> p m t", t=PACK),
+            d_picked[:].rearrange("p (m t) -> p m t", t=PACK),
+        )
+        x_picked = []
+        for c in range(2):
+            picked = keep.tile([P, HALF], U32, name="x_picked%d" % c, align_bytes=64)
+            nc.vector.tensor_copy(picked[:], x_word_table[:].indirect(offs_t[:, 16 * c : 16 * c + 16]))
+            x_picked.append(picked)
+
+        h = [keep.tile([P, S], F32, name="h%d" % t) for t in range(PACK)]
+        for t in range(PACK):
+            for c in range(2):
+                acc = psum.tile([P, HALF], F32, name="acc", tag="bank%d" % ((2 * t + c) if t < 2 else (2 * t + c - 3) % 4))
+                nc.tensor.matmul_mx(
+                    out=acc[:],
+                    lhsT=d_dealt[:, P * t : P * (t + 1)].bitcast(FP8X4),
+                    lhsT_scale=planes[:, P * t : P * (t + 1)],
+                    rhs=x_picked[c][:].bitcast(FP8X4),
+                    rhs_scale=planes[:, S + HALF * c : S + HALF * (c + 1)],
+                    start=True,
+                    stop=True,
+                )
+                cols = slice(HALF * c, HALF * (c + 1))
+                if c == 0 and t >= 2:
+                    nc.scalar.activation(h[t][:, cols], acc[:], ACT.Copy, scale=0.0625)
+                else:
+                    nc.vector.tensor_scalar(h[t][:, cols], acc[:], 0.0625, None, ALU.mult)
+
+        w_woven = keep.tile([P, PACK, P, PACK], BF16, name="w_woven", align_bytes=64)
+        w_codes = keep.tile([P, S], U32, name="w_codes", align_bytes=64)
+        w_scales = keep.tile([P, S], U8, name="w_scales", align_bytes=64)
+
+        def round_w(c):
+            nc.vector.tensor_copy(
+                w_woven[:, :, 64 * c : 64 * c + 64, :].rearrange("p t m j -> p m j t"),
+                w_raw[:, c, :, :].rearrange("p j (m t) -> p m j t", t=PACK),
+            )
+
+        def quantise_w(t):
+            nc.vector.quantize_mx(
+                out=w_codes[:, P * t : P * (t + 1)].bitcast(FP8X4),
+                scales=w_scales[:, P * t : P * (t + 1)],
+                in_=w_woven[:, t, :, :].rearrange("p m j -> p (m j)"),
+            )
+
+        z_codes = keep.tile([P, S], U32, name="z_codes", align_bytes=64)
+        z_scales = keep.tile([P, S], U8, name="z_scales", align_bytes=64)
+        gates = keep.tile([P, 3, HALF], F32, name="gates")
+        for c in range(2):
+            cols = slice(HALF * c, HALF * (c + 1))
+            z_rows = keep.tile([P, PACK, HALF], BF16, name="z_rows%d" % c, align_bytes=64)
+            z_woven = keep.tile([P, HALF, PACK], BF16, name="z_woven%d" % c, align_bytes=64)
+            for t in range(PACK):
+                gate = gates[:, (PACK * c + t) % 3, :]
+                nc.scalar.activation(gate, h[t][:].indirect(n1_t[:, 16 * c : 16 * c + 16]), ACT.Sigmoid)
+                nc.vector.scalar_tensor_tensor(
+                    z_rows[:, t, :], h[t][:, cols], gain[:, t : t + 1], gate, ALU.mult, ALU.mult
+                )
+                if c == 0 and t < 2:
+                    round_w(t)
+                if c == 0 and t == 2:
+                    quantise_w(0)
+            nc.vector.tensor_copy(
+                z_woven[:].rearrange("p (c i) t -> p c t i", i=4),
+                z_rows[:].rearrange("p t (c i) -> p c t i", i=4),
+            )
+            nc.vector.quantize_mx(
+                out=z_codes[:, cols].bitcast(FP8X4),
+                scales=z_scales[:, cols],
+                in_=z_woven[:].rearrange("p c t -> p (c t)"),
+            )
+
+        for t in range(1, PACK):
+            quantise_w(t)
+
+        out_rows = out.rearrange("(p t) n -> t p n", t=PACK)
+        h2 = [keep.tile([P, S], F32, name="h2_%d" % t) for t in range(PACK)]
+        pair = [keep.tile([P, 2 * PAIRS], F32, name="pair%d" % t) for t in range(PACK)]
+        squares = [keep.tile([P, 2 * PAIRS], F32, name="squares%d" % t) for t in range(PACK)]
+        radius2 = [keep.tile([P, PAIRS], F32, name="radius2_%d" % t) for t in range(PACK)]
+        radius = [keep.tile([P, PAIRS], F32, name="radius%d" % t) for t in range(PACK)]
+        result = [keep.tile([P, S], F32, name="result%d" % t) for t in range(PACK)]
+
+        def product(t, cols, bank):
+            acc = psum.tile([P, cols.stop - cols.start], F32, name="acc", tag="bank%d" % bank)
+            nc.tensor.matmul_mx(
+                out=acc[:],
+                lhsT=w_codes[:, P * t : P * (t + 1)].bitcast(FP8X4),
+                lhsT_scale=w_scales[:, P * t : P * (t + 1)],
+                rhs=z_codes[:, cols].bitcast(FP8X4),
+                rhs_scale=z_scales[:, cols],
+                start=True,
+                stop=True,
+            )
+            nc.scalar.copy(h2[t][:, cols], acc[:])
+
+        def fetch(t):
+            if t == 0:
+                product(t, slice(0, HALF), 4)
+                product(t, slice(HALF, S), 5)
+                nc.vector.tensor_scalar(pair[t][:, 0:PAIRS], h2[t][:].indirect(n2_t[:]), -0.5, 0.0, ALU.mult, ALU.add)
+            else:
+                product(t, slice(0, S), (5 + t) % 8)
+                nc.scalar.activation(pair[t][:, 0:PAIRS], h2[t][:].indirect(n2_t[:]), ACT.Copy, scale=-0.5)
+            nc.scalar.activation(pair[t][:, PAIRS:], h2[t][:].indirect(n3_t[:]), ACT.Copy)
+            nc.vector.tensor_tensor(result[t][:].indirect(n3_t[:]), pair[t][:, 0:PAIRS], pair[t][:, PAIRS:], ALU.add)
+
+        def square(t):
+            nc.scalar.activation(squares[t][:], pair[t][:], ACT.Square)
+            nc.vector.scalar_tensor_tensor(
+                radius2[t][:], squares[t][:, 0:PAIRS], 4.0, squares[t][:, PAIRS:], ALU.mult, ALU.add
+            )
+
+        def root(t):
+            nc.scalar.activation(radius[t][:], radius2[t][:], ACT.Sqrt, bias=0.25)
+            nc.vector.tensor_copy(result[t][:].indirect(n2_t[:]), radius[t][:])
+            nc.sync.dma_start(out_rows[t], result[t][:])
+
+        fetch(0)
+        square(0)
+        for t in range(1, PACK):
+            fetch(t)
+            if t == PACK - 1:
+                square(t)
+                root(t - 1)
+            else:
+                root(t - 1)
+                square(t)
+        root(PACK - 1)

@@ -19,6 +19,8 @@ S = 512
 PAIRS = 256
 HALF = 256
 
+CHUNKS = [slice(0, 256), slice(256, 384), slice(384, 512)]
+
 FLOPS = 2 * 2 * 512 * 512 * 512
 
 
@@ -43,19 +45,20 @@ def tile_picked_pqlaygatepolar_none_p_kernel(
         x_word_table = keep.tile([P, TABLE], U32, name="x_word_table", align_bytes=64)
         planes = keep.tile([P, 2 * S], U8, name="planes", align_bytes=64)
 
-        nc.vector.memset(d_byte_table[:].bitcast(I32), 0)
-        nc.gpsimd.memset(x_byte_table[:, 0 : TABLE // 2].bitcast(I32), 0)
-        nc.vector.memset(x_byte_table[:, TABLE // 2 :].bitcast(I32), 0)
         nc.gpsimd.memset(planes[:].bitcast(I32), 0)
 
-        nc.sync.dma_start(d_byte_table[0:P:8, :].bitcast(I32), d_scales[0].bitcast(I32))
-        nc.sync.dma_start(x_byte_table[0:P:8, :].bitcast(I32), x_scales[0].bitcast(I32))
+        warm = keep.tile([P, 32], F32, name="warm")
+        nc.gpsimd.memset(warm[:, 0:1], 0.0)
+        nc.scalar.activation(warm[:, 8:9], warm[:, 0:1], ACT.Sigmoid)
+        spread = [16, 8, TABLE // 4]
         nc.sync.dma_start(k1_t[:], k1)
+        nc.sync.dma_start(d_byte_table[:].bitcast(I32), d_scales[0].bitcast(I32).unsqueeze(1).broadcast_to(spread))
         nc.sync.dma_start(offs_t[:], offs)
+        nc.sync.dma_start(x_byte_table[:].bitcast(I32), x_scales[0].bitcast(I32).unsqueeze(1).broadcast_to(spread))
+        nc.sync.dma_start(d_word_table[:].bitcast(I32), d_words[0].rearrange("p n t -> p (n t)").bitcast(I32))
         nc.sync.dma_start(n1_t[:], n1)
         nc.sync.dma_start(n2_t[:], n2)
         nc.sync.dma_start(n3_t[:], n3)
-        nc.sync.dma_start(d_word_table[:].bitcast(I32), d_words[0].rearrange("p n t -> p (n t)").bitcast(I32))
         nc.sync.dma_start(x_word_table[:].bitcast(I32), x_words[0].rearrange("p n t -> p (n t)").bitcast(I32))
 
         d_bytes = keep.tile([P, S], U8, name="d_bytes", tag="early0", align_bytes=64)
@@ -64,8 +67,8 @@ def tile_picked_pqlaygatepolar_none_p_kernel(
         nc.vector.tensor_copy(d_bytes[:], d_byte_table[:].indirect(k1_t[:]))
         nc.vector.tensor_copy(x_bytes[:], x_byte_table[:].indirect(offs_t[:]))
         nc.vector.tensor_copy(
-            staged[:, 0:S].rearrange("p (t m) -> p m t", t=PACK),
-            d_bytes[:].rearrange("p (m t) -> p m t", t=PACK),
+            staged[:, 0:S].rearrange("p (t b i) -> p b t i", t=PACK, i=16),
+            d_bytes[:].rearrange("p (b i t) -> p b t i", t=PACK, i=16),
         )
         nc.vector.tensor_copy(staged[:, S : 2 * S].bitcast(I32), x_bytes[:].bitcast(I32))
         for q in range(4):
@@ -81,72 +84,85 @@ def tile_picked_pqlaygatepolar_none_p_kernel(
         gain = keep.tile([P, PACK], F32, name="gain", tag="early2", align_bytes=64)
         nc.sync.dma_start(gain[:], gn.rearrange("(p t) o -> p (t o)", t=PACK))
 
+
+        gain16 = keep.tile([P, PACK], F32, name="gain16")
+        nc.gpsimd.tensor_scalar(gain16[:], gain[:], 0.0625, 0.0, ALU.mult, ALU.add)
+
         d_picked = keep.tile([P, S], U32, name="d_picked", align_bytes=64)
         d_dealt = keep.tile([P, S], U32, name="d_dealt", align_bytes=64)
         nc.vector.tensor_copy(d_picked[:], d_word_table[:].indirect(k1_t[:]))
         nc.vector.tensor_copy(
-            d_dealt[:].rearrange("p (t m) -> p m t", t=PACK),
-            d_picked[:].rearrange("p (m t) -> p m t", t=PACK),
+            d_dealt[:].rearrange("p (t b i) -> p b t i", t=PACK, i=4),
+            d_picked[:].rearrange("p (b i t) -> p b t i", t=PACK, i=4),
         )
-        x_picked = []
+        x_picked = keep.tile([P, S], U32, name="x_picked", align_bytes=64)
         for c in range(2):
-            picked = keep.tile([P, HALF], U32, name="x_picked%d" % c, align_bytes=64)
-            nc.vector.tensor_copy(picked[:], x_word_table[:].indirect(offs_t[:, 16 * c : 16 * c + 16]))
-            x_picked.append(picked)
-
-        h = [keep.tile([P, S], F32, name="h%d" % t) for t in range(PACK)]
-        for t in range(PACK):
-            for c in range(2):
-                acc = psum.tile([P, HALF], F32, name="acc", tag="bank%d" % ((2 * t + c) if t < 2 else (2 * t + c - 3) % 4))
-                nc.tensor.matmul_mx(
-                    out=acc[:],
-                    lhsT=d_dealt[:, P * t : P * (t + 1)].bitcast(FP8X4),
-                    lhsT_scale=planes[:, P * t : P * (t + 1)],
-                    rhs=x_picked[c][:].bitcast(FP8X4),
-                    rhs_scale=planes[:, S + HALF * c : S + HALF * (c + 1)],
-                    start=True,
-                    stop=True,
-                )
-                cols = slice(HALF * c, HALF * (c + 1))
-                if c == 0 and t >= 2:
-                    nc.scalar.activation(h[t][:, cols], acc[:], ACT.Copy, scale=0.0625)
-                else:
-                    nc.vector.tensor_scalar(h[t][:, cols], acc[:], 0.0625, None, ALU.mult)
-
-        w_woven = keep.tile([P, PACK, P, PACK], BF16, name="w_woven", align_bytes=64)
-        w_codes = keep.tile([P, S], U32, name="w_codes", align_bytes=64)
-        w_scales = keep.tile([P, S], U8, name="w_scales", align_bytes=64)
-
-        def round_w(c):
             nc.vector.tensor_copy(
-                w_woven[:, :, 64 * c : 64 * c + 64, :].rearrange("p t m j -> p m j t"),
-                w_raw[:, c, :, :].rearrange("p j (m t) -> p m j t", t=PACK),
+                x_picked[:, HALF * c : HALF * (c + 1)], x_word_table[:].indirect(offs_t[:, 16 * c : 16 * c + 16])
             )
 
-        def quantise_w(t):
+        h = [keep.tile([P, S], F32, name="h%d" % t) for t in range(PACK)]
+        pieces = [(0, slice(0, HALF)), (0, slice(HALF, S))] + [(t, slice(0, S)) for t in range(1, PACK)]
+        sums = {}
+        for bank, (t, cols) in enumerate(pieces):
+            acc = psum.tile([P, cols.stop - cols.start], F32, name="acc", tag="bank%d" % bank)
+            nc.tensor.matmul_mx(
+                out=acc[:],
+                lhsT=d_dealt[:, P * t : P * (t + 1)].bitcast(FP8X4),
+                lhsT_scale=planes[:, P * t : P * (t + 1)],
+                rhs=x_picked[:, cols].bitcast(FP8X4),
+                rhs_scale=planes[:, S + cols.start : S + cols.stop],
+                start=True,
+                stop=True,
+            )
+            for c, chunk in enumerate(CHUNKS):
+                if cols.start <= chunk.start and chunk.stop <= cols.stop:
+                    sums[t, c] = acc[:, chunk.start - cols.start : chunk.stop - cols.start]
+            if bank == 0:
+                nc.scalar.activation(h[t][:, cols], acc[:], ACT.Copy, scale=0.0625)
+            else:
+                nc.vector.tensor_scalar(h[t][:, cols], acc[:], 0.0625, None, ALU.mult)
+
+        w_woven = keep.tile([P, PACK, P, PACK], BF16, name="w_woven", align_bytes=64)
+        w_scales = keep.tile([P, S], U8, name="w_scales", align_bytes=64)
+        w_first = keep.tile([P, P], U32, name="w_first", align_bytes=64)
+
+        def round_w(c):
+            nc.gpsimd.tensor_scalar(
+                w_woven[:, :, 64 * c : 64 * c + 64, :].rearrange("p t m j -> p m t j"),
+                w_raw[:, c, :, :].rearrange("p j (m t) -> p m t j", t=PACK),
+                1.0,
+                0.0,
+                ALU.mult,
+                ALU.add,
+            )
+
+        def quantise_w(codes, t0, t1):
             nc.vector.quantize_mx(
-                out=w_codes[:, P * t : P * (t + 1)].bitcast(FP8X4),
-                scales=w_scales[:, P * t : P * (t + 1)],
-                in_=w_woven[:, t, :, :].rearrange("p m j -> p (m j)"),
+                out=codes.bitcast(FP8X4),
+                scales=w_scales[:, P * t0 : P * t1],
+                in_=w_woven[:, t0:t1, :, :].rearrange("p t m j -> p (t m j)"),
             )
 
         z_codes = keep.tile([P, S], U32, name="z_codes", align_bytes=64)
         z_scales = keep.tile([P, S], U8, name="z_scales", align_bytes=64)
-        gates = keep.tile([P, 3, HALF], F32, name="gates")
-        for c in range(2):
-            cols = slice(HALF * c, HALF * (c + 1))
-            z_rows = keep.tile([P, PACK, HALF], BF16, name="z_rows%d" % c, align_bytes=64)
-            z_woven = keep.tile([P, HALF, PACK], BF16, name="z_woven%d" % c, align_bytes=64)
+        gates = keep.tile([P, PACK, HALF], F32, name="gates")
+        for c, cols in enumerate(CHUNKS):
+            width = cols.stop - cols.start
+            z_rows = keep.tile([P, PACK, width], BF16, name="z_rows", tag="z_rows%d" % c, align_bytes=64)
+            z_woven = keep.tile([P, width, PACK], BF16, name="z_woven", tag="z_woven%d" % c, align_bytes=64)
             for t in range(PACK):
-                gate = gates[:, (PACK * c + t) % 3, :]
-                nc.scalar.activation(gate, h[t][:].indirect(n1_t[:, 16 * c : 16 * c + 16]), ACT.Sigmoid)
+                gate = gates[:, t, 0:width]
+                nc.scalar.activation(
+                    gate, h[t][:].indirect(n1_t[:, cols.start // 16 : cols.stop // 16]), ACT.Sigmoid
+                )
                 nc.vector.scalar_tensor_tensor(
-                    z_rows[:, t, :], h[t][:, cols], gain[:, t : t + 1], gate, ALU.mult, ALU.mult
+                    z_rows[:, t, :], sums[t, c], gain16[:, t : t + 1], gate, ALU.mult, ALU.mult
                 )
                 if c == 0 and t < 2:
                     round_w(t)
-                if c == 0 and t == 2:
-                    quantise_w(0)
+                if c == 1 and t == 0:
+                    quantise_w(w_first[:], 0, 1)
             nc.vector.tensor_copy(
                 z_woven[:].rearrange("p (c i) t -> p c t i", i=4),
                 z_rows[:].rearrange("p t (c i) -> p c t i", i=4),
@@ -157,8 +173,10 @@ def tile_picked_pqlaygatepolar_none_p_kernel(
                 in_=z_woven[:].rearrange("p c t -> p (c t)"),
             )
 
-        for t in range(1, PACK):
-            quantise_w(t)
+        nc.scalar.activation(warm[:, 16:17], gates[:, PACK - 1, 0:1], ACT.Sqrt)
+        w_rest = keep.tile([P, S - P], U32, name="w_rest", tag="z_woven2", align_bytes=64)
+        quantise_w(w_rest[:], 1, PACK)
+        w_codes = [w_first[:]] + [w_rest[:, P * t : P * (t + 1)] for t in range(PACK - 1)]
 
         out_rows = out.rearrange("(p t) n -> t p n", t=PACK)
         h2 = [keep.tile([P, S], F32, name="h2_%d" % t) for t in range(PACK)]
@@ -172,7 +190,7 @@ def tile_picked_pqlaygatepolar_none_p_kernel(
             acc = psum.tile([P, cols.stop - cols.start], F32, name="acc", tag="bank%d" % bank)
             nc.tensor.matmul_mx(
                 out=acc[:],
-                lhsT=w_codes[:, P * t : P * (t + 1)].bitcast(FP8X4),
+                lhsT=w_codes[t].bitcast(FP8X4),
                 lhsT_scale=w_scales[:, P * t : P * (t + 1)],
                 rhs=z_codes[:, cols].bitcast(FP8X4),
                 rhs_scale=z_scales[:, cols],
@@ -183,20 +201,20 @@ def tile_picked_pqlaygatepolar_none_p_kernel(
 
         def fetch(t):
             if t == 0:
-                product(t, slice(0, HALF), 4)
-                product(t, slice(HALF, S), 5)
+                for c, cols in enumerate(CHUNKS):
+                    product(t, cols, 5 + c)
                 nc.vector.tensor_scalar(pair[t][:, 0:PAIRS], h2[t][:].indirect(n2_t[:]), -0.5, 0.0, ALU.mult, ALU.add)
             else:
-                product(t, slice(0, S), (5 + t) % 8)
+                product(t, slice(0, S), 0 if t == 1 else t)
                 nc.scalar.activation(pair[t][:, 0:PAIRS], h2[t][:].indirect(n2_t[:]), ACT.Copy, scale=-0.5)
             nc.scalar.activation(pair[t][:, PAIRS:], h2[t][:].indirect(n3_t[:]), ACT.Copy)
             nc.vector.tensor_tensor(result[t][:].indirect(n3_t[:]), pair[t][:, 0:PAIRS], pair[t][:, PAIRS:], ALU.add)
 
         def square(t):
-            nc.scalar.activation(squares[t][:], pair[t][:], ACT.Square)
-            nc.vector.scalar_tensor_tensor(
-                radius2[t][:], squares[t][:, 0:PAIRS], 4.0, squares[t][:, PAIRS:], ALU.mult, ALU.add
-            )
+            nc.scalar.activation(squares[t][:, 0:PAIRS], pair[t][:, 0:PAIRS], ACT.Square, scale=2.0)
+            nc.scalar.activation(squares[t][:, PAIRS:], pair[t][:, PAIRS:], ACT.Square)
+            adder = nc.vector if t == 0 else nc.gpsimd
+            adder.tensor_tensor(radius2[t][:], squares[t][:, 0:PAIRS], squares[t][:, PAIRS:], ALU.add)
 
         def root(t):
             nc.scalar.activation(radius[t][:], radius2[t][:], ACT.Sqrt, bias=0.25)

from contextlib import ExitStack

import concourse.mybir as mybir

F32 = mybir.dt.float32
BF16 = mybir.dt.bfloat16
I32 = mybir.dt.int32
U32 = mybir.dt.uint32
U16 = mybir.dt.uint16
U8 = mybir.dt.uint8
FP8X4 = mybir.dt.float8_e4m3fn_x4
ACT = mybir.ActivationFunctionType
ALU = mybir.AluOpType

P = 128
PACK = 4
TABLE = 2048
S = 512
PAIRS = 256
HALF = 256

CHUNKS = [slice(0, 256), slice(256, 384), slice(384, 512)]

FLOPS = 2 * 2 * 512 * 512 * 512


def tile_picked_pqlaygatepolar_none_p_kernel(
    tc, x_words, x_scales, d_words, d_scales, gn, w1, offs, k1, n1, n2, n3, out
):
    nc = tc.nc
    with ExitStack() as ctx:
        lists = ctx.enter_context(tc.tile_pool(name="lists", bufs=1))
        keep = ctx.enter_context(tc.tile_pool(name="keep", bufs=1))
        psum = ctx.enter_context(tc.psum_pool(name="psum", bufs=1))

        k1_t = lists.tile([P, S // 16], U16, name="k1_t")
        offs_t = lists.tile([P, S // 16], U16, name="offs_t")
        n1_t = lists.tile([P, S // 16], U16, name="n1_t")
        n2_t = lists.tile([P, PAIRS // 16], U16, name="n2_t")
        n3_t = lists.tile([P, PAIRS // 16], U16, name="n3_t")

        d_byte_table = keep.tile([P, TABLE], U8, name="d_byte_table", tag="early2", align_bytes=64)
        x_byte_table = keep.tile([P, TABLE], U8, name="x_byte_table", align_bytes=64)
        d_word_table = keep.tile([P, TABLE], U32, name="d_word_table", align_bytes=64)
        x_word_table = keep.tile([P, TABLE], U32, name="x_word_table", align_bytes=64)
        planes = keep.tile([P, 2 * S], U8, name="planes", align_bytes=64)

        nc.gpsimd.memset(planes[:].bitcast(I32), 0)

        warm = keep.tile([P, 32], F32, name="warm")
        nc.gpsimd.memset(warm[:, 0:1], 0.0)
        nc.scalar.activation(warm[:, 8:9], warm[:, 0:1], ACT.Sigmoid)
        spread = [16, 8, TABLE // 4]
        nc.sync.dma_start(k1_t[:], k1)
        nc.sync.dma_start(d_byte_table[:].bitcast(I32), d_scales[0].bitcast(I32).unsqueeze(1).broadcast_to(spread))
        nc.sync.dma_start(offs_t[:], offs)
        nc.sync.dma_start(x_byte_table[:].bitcast(I32), x_scales[0].bitcast(I32).unsqueeze(1).broadcast_to(spread))
        nc.sync.dma_start(d_word_table[:].bitcast(I32), d_words[0].rearrange("p n t -> p (n t)").bitcast(I32))
        nc.sync.dma_start(n1_t[:], n1)
        nc.sync.dma_start(n2_t[:], n2)
        nc.sync.dma_start(n3_t[:], n3)
        nc.sync.dma_start(x_word_table[:].bitcast(I32), x_words[0].rearrange("p n t -> p (n t)").bitcast(I32))

        d_bytes = keep.tile([P, S], U8, name="d_bytes", tag="early0", align_bytes=64)
        x_bytes = keep.tile([P, S], U8, name="x_bytes", tag="early1", align_bytes=64)
        staged = keep.tile([P, 2 * S], U8, name="staged", align_bytes=64)
        nc.vector.tensor_copy(d_bytes[:], d_byte_table[:].indirect(k1_t[:]))
        nc.vector.tensor_copy(x_bytes[:], x_byte_table[:].indirect(offs_t[:]))
        nc.vector.tensor_copy(
            staged[:, 0:S].rearrange("p (t b i) -> p b t i", t=PACK, i=16),
            d_bytes[:].rearrange("p (b i t) -> p b t i", t=PACK, i=16),
        )
        nc.vector.tensor_copy(staged[:, S : 2 * S].bitcast(I32), x_bytes[:].bitcast(I32))
        for q in range(4):
            (nc.sync if q % 2 == 0 else nc.scalar).dma_start(
                planes[32 * q : 32 * q + 4, :].bitcast(I32),
                staged[32 * q : 32 * q + 32 : 8, :].bitcast(I32),
            )

        w_rows = w1.rearrange("(p j) n -> p j n", j=PACK)
        w_raw = keep.tile([P, 2, PACK, HALF], F32, name="w_raw", tag="early1", align_bytes=64)
        for c in range(2):
            nc.sync.dma_start(w_raw[:, c, :, :], w_rows[:, :, HALF * c : HALF * (c + 1)])
        gain = keep.tile([P, PACK], F32, name="gain", tag="early2", align_bytes=64)
        nc.sync.dma_start(gain[:], gn.rearrange("(p t) o -> p (t o)", t=PACK))


        gain16 = keep.tile([P, PACK], F32, name="gain16")
        nc.gpsimd.tensor_scalar(gain16[:], gain[:], 0.0625, 0.0, ALU.mult, ALU.add)

        d_picked = keep.tile([P, S], U32, name="d_picked", align_bytes=64)
        d_dealt = keep.tile([P, S], U32, name="d_dealt", align_bytes=64)
        nc.vector.tensor_copy(d_picked[:], d_word_table[:].indirect(k1_t[:]))
        nc.vector.tensor_copy(
            d_dealt[:].rearrange("p (t b i) -> p b t i", t=PACK, i=4),
            d_picked[:].rearrange("p (b i t) -> p b t i", t=PACK, i=4),
        )
        x_picked = keep.tile([P, S], U32, name="x_picked", align_bytes=64)
        for c in range(2):
            nc.vector.tensor_copy(
                x_picked[:, HALF * c : HALF * (c + 1)], x_word_table[:].indirect(offs_t[:, 16 * c : 16 * c + 16])
            )

        h = [keep.tile([P, S], F32, name="h%d" % t) for t in range(PACK)]
        pieces = [(0, slice(0, HALF)), (0, slice(HALF, S))] + [(t, slice(0, S)) for t in range(1, PACK)]
        sums = {}
        for bank, (t, cols) in enumerate(pieces):
            acc = psum.tile([P, cols.stop - cols.start], F32, name="acc", tag="bank%d" % bank)
            nc.tensor.matmul_mx(
                out=acc[:],
                lhsT=d_dealt[:, P * t : P * (t + 1)].bitcast(FP8X4),
                lhsT_scale=planes[:, P * t : P * (t + 1)],
                rhs=x_picked[:, cols].bitcast(FP8X4),
                rhs_scale=planes[:, S + cols.start : S + cols.stop],
                start=True,
                stop=True,
            )
            for c, chunk in enumerate(CHUNKS):
                if cols.start <= chunk.start and chunk.stop <= cols.stop:
                    sums[t, c] = acc[:, chunk.start - cols.start : chunk.stop - cols.start]
            if bank == 0:
                nc.scalar.activation(h[t][:, cols], acc[:], ACT.Copy, scale=0.0625)
            else:
                nc.vector.tensor_scalar(h[t][:, cols], acc[:], 0.0625, None, ALU.mult)

        w_woven = keep.tile([P, PACK, P, PACK], BF16, name="w_woven", align_bytes=64)
        w_scales = keep.tile([P, S], U8, name="w_scales", align_bytes=64)
        w_first = keep.tile([P, P], U32, name="w_first", align_bytes=64)

        def round_w(c):
            nc.gpsimd.tensor_scalar(
                w_woven[:, :, 64 * c : 64 * c + 64, :].rearrange("p t m j -> p m t j"),
                w_raw[:, c, :, :].rearrange("p j (m t) -> p m t j", t=PACK),
                1.0,
                0.0,
                ALU.mult,
                ALU.add,
            )

        def quantise_w(codes, t0, t1):
            nc.vector.quantize_mx(
                out=codes.bitcast(FP8X4),
                scales=w_scales[:, P * t0 : P * t1],
                in_=w_woven[:, t0:t1, :, :].rearrange("p t m j -> p (t m j)"),
            )

        z_codes = keep.tile([P, S], U32, name="z_codes", align_bytes=64)
        z_scales = keep.tile([P, S], U8, name="z_scales", align_bytes=64)
        gates = keep.tile([P, PACK, HALF], F32, name="gates")
        for c, cols in enumerate(CHUNKS):
            width = cols.stop - cols.start
            z_rows = keep.tile([P, PACK, width], BF16, name="z_rows", tag="z_rows%d" % c, align_bytes=64)
            z_woven = keep.tile([P, width, PACK], BF16, name="z_woven", tag="z_woven%d" % c, align_bytes=64)
            for t in range(PACK):
                gate = gates[:, t, 0:width]
                nc.scalar.activation(
                    gate, h[t][:].indirect(n1_t[:, cols.start // 16 : cols.stop // 16]), ACT.Sigmoid
                )
                nc.vector.scalar_tensor_tensor(
                    z_rows[:, t, :], sums[t, c], gain16[:, t : t + 1], gate, ALU.mult, ALU.mult
                )
                if c == 0 and t < 2:
                    round_w(t)
                if c == 1 and t == 0:
                    quantise_w(w_first[:], 0, 1)
            nc.vector.tensor_copy(
                z_woven[:].rearrange("p (c i) t -> p c t i", i=4),
                z_rows[:].rearrange("p t (c i) -> p c t i", i=4),
            )
            nc.vector.quantize_mx(
                out=z_codes[:, cols].bitcast(FP8X4),
                scales=z_scales[:, cols],
                in_=z_woven[:].rearrange("p c t -> p (c t)"),
            )

        nc.scalar.activation(warm[:, 16:17], gates[:, PACK - 1, 0:1], ACT.Sqrt)
        w_rest = keep.tile([P, S - P], U32, name="w_rest", tag="z_woven2", align_bytes=64)
        quantise_w(w_rest[:], 1, PACK)
        w_codes = [w_first[:]] + [w_rest[:, P * t : P * (t + 1)] for t in range(PACK - 1)]

        out_rows = out.rearrange("(p t) n -> t p n", t=PACK)
        h2 = [keep.tile([P, S], F32, name="h2_%d" % t) for t in range(PACK)]
        pair = [keep.tile([P, 2 * PAIRS], F32, name="pair%d" % t) for t in range(PACK)]
        squares = [keep.tile([P, 2 * PAIRS], F32, name="squares%d" % t) for t in range(PACK)]
        radius2 = [keep.tile([P, PAIRS], F32, name="radius2_%d" % t) for t in range(PACK)]
        radius = [keep.tile([P, PAIRS], F32, name="radius%d" % t) for t in range(PACK)]
        result = [keep.tile([P, S], F32, name="result%d" % t) for t in range(PACK)]

        def product(t, cols, bank):
            acc = psum.tile([P, cols.stop - cols.start], F32, name="acc", tag="bank%d" % bank)
            nc.tensor.matmul_mx(
                out=acc[:],
                lhsT=w_codes[t].bitcast(FP8X4),
                lhsT_scale=w_scales[:, P * t : P * (t + 1)],
                rhs=z_codes[:, cols].bitcast(FP8X4),
                rhs_scale=z_scales[:, cols],
                start=True,
                stop=True,
            )
            nc.scalar.copy(h2[t][:, cols], acc[:])

        def fetch(t):
            if t == 0:
                for c, cols in enumerate(CHUNKS):
                    product(t, cols, 5 + c)
                nc.vector.tensor_scalar(pair[t][:, 0:PAIRS], h2[t][:].indirect(n2_t[:]), -0.5, 0.0, ALU.mult, ALU.add)
            else:
                product(t, slice(0, S), 0 if t == 1 else t)
                nc.scalar.activation(pair[t][:, 0:PAIRS], h2[t][:].indirect(n2_t[:]), ACT.Copy, scale=-0.5)
            nc.scalar.activation(pair[t][:, PAIRS:], h2[t][:].indirect(n3_t[:]), ACT.Copy)
            nc.vector.tensor_tensor(result[t][:].indirect(n3_t[:]), pair[t][:, 0:PAIRS], pair[t][:, PAIRS:], ALU.add)

        def square(t):
            nc.scalar.activation(squares[t][:, 0:PAIRS], pair[t][:, 0:PAIRS], ACT.Square, scale=2.0)
            nc.scalar.activation(squares[t][:, PAIRS:], pair[t][:, PAIRS:], ACT.Square)
            adder = nc.vector if t == 0 else nc.gpsimd
            adder.tensor_tensor(radius2[t][:], squares[t][:, 0:PAIRS], squares[t][:, PAIRS:], ALU.add)

        def root(t):
            nc.scalar.activation(radius[t][:], radius2[t][:], ACT.Sqrt, bias=0.25)
            nc.vector.tensor_copy(result[t][:].indirect(n2_t[:]), radius[t][:])
            nc.sync.dma_start(out_rows[t], result[t][:])

        fetch(0)
        square(0)
        for t in range(1, PACK):
            fetch(t)
            if t == PACK - 1:
                square(t)
                root(t - 1)
            else:
                root(t - 1)
                square(t)
        root(PACK - 1)
